import numpy as np
import ml_dtypes


def mxq(x, axis, fmt="e4m3"):
    dtype, down = {"e4m3": (ml_dtypes.float8_e4m3fn, 7), "e5m2": (ml_dtypes.float8_e5m2, 14)}[fmt]
    v = np.moveaxis(np.asarray(x, np.float32).astype(ml_dtypes.bfloat16).astype(np.float64), axis, -1)
    blocks = v.reshape(v.shape[:-1] + (-1, 32))
    amax = np.abs(blocks).max(-1, keepdims=True)
    byte = np.maximum(np.where(amax > 0, np.frexp(amax)[1] - 1 + 127, 0) - down, 1)
    scale = np.exp2(byte - 127.0)
    codes = (blocks / scale).astype(np.float32).astype(dtype).astype(np.float64)
    return np.moveaxis((codes * scale).reshape(v.shape), -1, axis)


WIDE = False


def mx_kscale(k):
    if not WIDE:
        return np.ones(k)
    levels = np.array([10, -10, 5, -5, 0])
    if k % 512:
        return np.exp2(np.random.permutation(np.resize(levels, k // 32))).repeat(32)
    a = np.empty((k // 512, 16))
    for p in range(k // 512):
        a[p, :8] = np.random.permutation(np.resize(levels, 8))
        for g in range(8):
            far = levels[np.abs(levels - a[p, g]) >= 10]
            a[p, g + 8] = far[np.random.randint(len(far))]
    return np.exp2(a.ravel()).repeat(32)


BF16 = ml_dtypes.bfloat16


def bf(x):
    return np.asarray(x, np.float32).astype(BF16)


def f64(x):
    return np.asarray(x).astype(np.float64)


B, T, U, E, P, J, V = 16, 16, 8, 512, 512, 512, 512


def _log_normalize(x):
    m = np.max(x, axis=-1, keepdims=True)
    lse = m + np.log(np.sum(np.exp(x - m), axis=-1, keepdims=True))
    return x - lse


def _softplus(z):
    return np.maximum(z, 0.0) + np.log(1.0 + np.exp(-np.abs(z)))


def draw0():
    se, sp, sj = mx_kscale(E), mx_kscale(P), mx_kscale(J)
    return {
        "enc": bf(np.random.standard_normal((B, T, E)) * se),
        "pred": bf(np.random.standard_normal((B, U, P)) * sp),
        "we": bf(np.random.standard_normal((E, J)) / np.sqrt(E) / se[:, None]),
        "wp": bf(np.random.standard_normal((P, J)) / np.sqrt(P) / sp[:, None]),
        "gj": bf((1.0 + 0.2 * np.random.standard_normal(J)) * sj),
        "wo": bf(np.random.standard_normal((J, V)) * 3.0 / np.sqrt(J) / sj[:, None]),
        "wb": bf(np.random.standard_normal(J) * 2.0 / np.sqrt(J)),
    }


def core(enc, pred, we, wp, gj, wo, wb):
    f = mxq(f64(enc), 2, "e4m3") @ mxq(f64(we), 0, "e4m3")
    g = mxq(f64(pred), 2, "e4m3") @ mxq(f64(wp), 0, "e4m3")
    t = np.tanh(f[:, :, None, :] + g[:, None, :, :])
    h = t * f64(gj)[None, None, None, :]
    logits = mxq(h, 3, "e4m3") @ mxq(f64(wo), 0, "e4m3")
    ls = _log_normalize(logits)
    zb = np.sum(t * f64(wb)[None, None, None, :], axis=-1)
    return ls - _softplus(zb)[:, :, :, None]


def e4m3fn_bytes(y):
    return np.clip(np.asarray(y, np.float64), -448.0, 448.0).astype(np.float32).astype(ml_dtypes.float8_e4m3fn).view(np.uint8)


def e4m3fn_values(b):
    return np.asarray(b, np.uint8).view(ml_dtypes.float8_e4m3fn).astype(np.float64)


def setup_inputs():
    d = draw0()
    x0 = np.asarray(d['wp']).astype(np.float64)
    s = (np.max(np.abs(x0), axis=(1,), keepdims=True) / 448.0).astype(np.float32)
    out = {}
    for k, v in d.items():
        if k == 'wp':
            out['wp_bytes'] = e4m3fn_bytes(x0 / s.astype(np.float64))
            out['wp_scale'] = s
        else:
            out[k] = v
    return out


def reference(enc, pred, we, wp_bytes, wp_scale, gj, wo, wb):
    return core(enc, pred, we, e4m3fn_values(wp_bytes) * wp_scale.astype(np.float64), gj, wo, wb)

@@ -1,0 +1,632 @@
+from contextlib import ExitStack
+
+import concourse.mybir as mybir
+from concourse.masks import make_identity
+
+F32 = mybir.dt.float32
+BF16 = mybir.dt.bfloat16
+I32 = mybir.dt.int32
+U8 = mybir.dt.uint8
+FP8 = mybir.dt.float8_e4m3fn
+FP8X4 = mybir.dt.float8_e4m3fn_x4
+ALU = mybir.AluOpType
+ACT = mybir.ActivationFunctionType
+
+P = 128
+LN2 = 0.6931471805599453
+B, T, U, K, J, V = 16, 16, 8, 512, 512, 512
+ROWS = B * T * U
+PAIRS = B // 2
+
+FLOPS = 2 * K * J * (B * T + B * U) + 2 * ROWS * J * V + 2 * ROWS * J
+
+
+def tile_hybridautoregressivetransducerjoiner_kernel(
+    tc, enc, pred, we, wp_bytes, wp_scale, gj, wo, wb, out
+):
+    nc = tc.nc
+
+    with ExitStack() as ctx:
+        keep = ctx.enter_context(tc.tile_pool(name="keep", bufs=1))
+        work = ctx.enter_context(tc.tile_pool(name="work", bufs=3))
+        psum = ctx.enter_context(tc.psum_pool(name="psum", bufs=1))
+        ctx.enter_context(tc.manual_schedule())
+
+        wp_raw = keep.tile([P, 4, J], U8, align_bytes=64)
+        nc.sync.dma_start(out=wp_raw[:], in_=wp_bytes.rearrange("(p j) n -> p j n", j=4))
+        pred_raw = keep.tile([P, K], BF16, align_bytes=64)
+        nc.sync.dma_start(out=pred_raw[:], in_=pred.rearrange("b u k -> (b u) k"))
+        enc_raw = keep.tile([P, 2, K], BF16, align_bytes=64)
+        nc.sync.dma_start(out=enc_raw[:], in_=enc.rearrange("b i k -> (b i) k").rearrange("(p e) k -> p e k", e=2))
+        we_raw = keep.tile([P, 4, J], BF16, align_bytes=64)
+        nc.sync.dma_start(out=we_raw[:], in_=we.rearrange("(p j) n -> p j n", j=4))
+        wo_raw = keep.tile([P, 4, V], BF16, align_bytes=64)
+        nc.sync.dma_start(out=wo_raw[:], in_=wo.rearrange("(p j) n -> p j n", j=4))
+        wps = keep.tile([P, 4], F32)
+        nc.scalar.dma_start(out=wps[:], in_=wp_scale.rearrange("(p j) o -> p (j o)", j=4))
+        gj_raw = keep.tile([P, 4], BF16)
+        nc.scalar.dma_start(out=gj_raw[:], in_=gj.rearrange("(p t) -> p t", t=4))
+        wb_raw = keep.tile([P, 4], BF16)
+        nc.scalar.dma_start(out=wb_raw[:], in_=wb.rearrange("(p t) -> p t", t=4))
+
+        warm = keep.tile([P, 1], F32)
+        nc.vector.memset(warm[:], 0.0)
+        warm_out = keep.tile([P, 1], F32)
+        nc.scalar.activation(out=warm_out[:], in_=warm[:], func=ACT.Exp)
+        minus_one = keep.tile([P, 1], F32)
+        nc.gpsimd.memset(minus_one[:], -1.0)
+        ident = keep.tile([P, P], F32)
+        make_identity(nc, ident[:])
+        enc_s = keep.tile([P, B * T], U8, align_bytes=64)
+        nc.gpsimd.memset(enc_s[:].bitcast(I32), 0)
+        pred_s = keep.tile([P, B * U * 4], U8, align_bytes=64)
+        nc.gpsimd.memset(pred_s[:].bitcast(I32), 0)
+        gain = keep.tile([P, 4], F32)
+        nc.gpsimd.tensor_copy(out=gain[:], in_=gj_raw[:])
+        wbf = keep.tile([P, 4], F32)
+        nc.gpsimd.tensor_copy(out=wbf[:], in_=wb_raw[:])
+
+        enc_g = keep.tile([P, B * T * 4], BF16, align_bytes=64)
+        pred_g = keep.tile([P, B * U * 16], BF16, align_bytes=64)
+        enc_c = keep.tile([P, B * T], I32, align_bytes=64)
+        pred_c = keep.tile([P, B * U * 4], I32, align_bytes=64)
+        wp_w = keep.tile([P, 4, J], BF16, align_bytes=64)
+        xs = {}
+
+        def copy(eng, out, in_):
+            if eng == "V":
+                nc.vector.tensor_copy(out=out, in_=in_)
+            else:
+                nc.scalar.copy(out=out, in_=in_)
+
+        def transpose_enc():
+            xe = psum.tile([P, 2, 2, P], F32, tag="s1", bufs=4)
+            for e in range(2):
+                words = enc_raw[:, e, :].bitcast(F32)
+                for u in range(2):
+                    nc.tensor.transpose(xe[:, e, u, :], words[:, u : K // 2 : 2], ident[:])
+            xs["e"] = xe
+
+        def transpose_pred():
+            xp = psum.tile([P, 2, P], F32, tag="lg", bufs=3)
+            pwords = pred_raw[:].bitcast(F32)
+            for u in range(2):
+                nc.tensor.transpose(xp[:, u, :], pwords[:, u : K // 2 : 2], ident[:])
+            xs["p"] = xp
+
+        def copy_enc(eng):
+            copy(
+                eng,
+                enc_g[:].bitcast(F32).rearrange("q (r e u) -> q r e u", e=2, u=2),
+                xs["e"][:].rearrange("q e u r -> q r e u"),
+            )
+
+        def copy_pred(eng):
+            copy(
+                eng,
+                pred_g[:].bitcast(F32).rearrange("q (r l u) -> q r l u", l=4, u=2),
+                xs["p"][:].rearrange("q u r -> q r u").unsqueeze(2).to_broadcast([P, P, 4, 2]),
+            )
+
+        def widen(eng, j):
+            if eng == "V":
+                nc.vector.tensor_scalar(
+                    out=wp_w[:, j, :],
+                    in0=wp_raw[:, j, :].bitcast(FP8),
+                    scalar1=wps[:, j : j + 1],
+                    scalar2=None,
+                    op0=ALU.mult,
+                )
+            else:
+                nc.scalar.activation(
+                    out=wp_w[:, j, :], in_=wp_raw[:, j, :].bitcast(FP8), func=ACT.Copy, scale=wps[:, j : j + 1]
+                )
+
+        enc_rc = keep.tile([P, ROWS], I32, align_bytes=64)
+        enc_rs = keep.tile([P, ROWS], U8, align_bytes=64)
+        pred_rc = keep.tile([P, ROWS], I32, align_bytes=64)
+        pred_rs = keep.tile([P, ROWS], U8, align_bytes=64)
+
+        def replicate(b0, nb):
+            nc.vector.tensor_copy(
+                out=enc_rc[:, b0 * 128 : (b0 + nb) * 128].rearrange("p (a u l) -> p a u l", u=8, l=4),
+                in_=enc_c[:, b0 * 16 : (b0 + nb) * 16]
+                .rearrange("p (a l) -> p a l", l=4)
+                .unsqueeze(2)
+                .to_broadcast([P, nb * 4, 8, 4]),
+            )
+            nc.vector.tensor_copy(
+                out=enc_rs[:].bitcast(I32)[:, b0 * 32 : (b0 + nb) * 32].rearrange("p (a u) -> p a u", u=8),
+                in_=enc_s[:].bitcast(I32)[:, b0 * 4 : (b0 + nb) * 4].unsqueeze(2).to_broadcast([P, nb * 4, 8]),
+            )
+            nc.vector.tensor_copy(
+                out=pred_rc[:, b0 * 128 : (b0 + nb) * 128].rearrange("p (b i w) -> p b i w", i=4, w=32),
+                in_=pred_c[:, b0 * 32 : (b0 + nb) * 32]
+                .rearrange("p (b w) -> p b w", w=32)
+                .unsqueeze(2)
+                .to_broadcast([P, nb, 4, 32]),
+            )
+            nc.vector.tensor_copy(
+                out=pred_rs[:].bitcast(I32)[:, b0 * 32 : (b0 + nb) * 32].rearrange("p (b i u) -> p b i u", i=4, u=8),
+                in_=pred_s[:]
+                .bitcast(I32)[:, b0 * 8 : (b0 + nb) * 8]
+                .rearrange("p (b u) -> p b u", u=8)
+                .unsqueeze(2)
+                .to_broadcast([P, nb, 4, 8]),
+            )
+
+        we_g = keep.tile([P, 4 * J], BF16, align_bytes=64)
+        wp_g = keep.tile([P, 4 * J], BF16, align_bytes=64)
+        we_c = keep.tile([P, J], I32, align_bytes=64)
+        we_s = keep.tile([P, J], U8, align_bytes=64)
+        wp_c = keep.tile([P, J], I32, align_bytes=64)
+        wp_s = keep.tile([P, J], U8, align_bytes=64)
+        wo_g = keep.tile([P, 4 * V], BF16, align_bytes=64)
+        wo_c = keep.tile([P, V], I32, align_bytes=64)
+        wo_s = keep.tile([P, V], U8, align_bytes=64)
+
+        def half_grouped(grouped, h):
+            return grouped[:, h * 1024 : (h + 1) * 1024].rearrange("p (t m j) -> p t m j", t=2, j=4)
+
+        def half_raw(raw, h):
+            return raw[:].rearrange("p j (m t) -> p t m j", t=4)[:, 2 * h : 2 * h + 2]
+
+        def quantize_half(grouped, codes, scales, h):
+            nc.vector.quantize_mx(
+                out=codes[:, h * 256 : (h + 1) * 256].bitcast(FP8X4),
+                scales=scales[:, h * 256 : (h + 1) * 256],
+                in_=grouped[:, h * 1024 : (h + 1) * 1024],
+            )
+
+        tts = []
+        for k in range(PAIRS):
+            tt = keep.tile([P, 4, 256], F32, tag="tt", bufs=PAIRS, align_bytes=64)
+            tts.append(tt)
+
+        s1s = {}
+
+        def first_stage(k, h):
+            s1 = psum.tile([P, 2, 256], F32, tag="s1", bufs=4)
+            s1s[(k, h)] = s1
+            cols = slice(k * 256, (k + 1) * 256)
+            for i in range(2):
+                t = 2 * h + i
+                ch = slice(t * 128, (t + 1) * 128)
+                nc.tensor.matmul_mx(
+                    out=s1[:, i, :],
+                    lhsT=we_c[:, ch].bitcast(FP8X4),
+                    lhsT_scale=we_s[:, ch],
+                    rhs=enc_rc[:, cols].bitcast(FP8X4),
+                    rhs_scale=enc_rs[:, cols],
+                    start=True,
+                    stop=False,
+                )
+                nc.tensor.matmul_mx(
+                    out=s1[:, i, :],
+                    lhsT=wp_c[:, ch].bitcast(FP8X4),
+                    lhsT_scale=wp_s[:, ch],
+                    rhs=pred_rc[:, cols].bitcast(FP8X4),
+                    rhs_scale=pred_rs[:, cols],
+                    start=False,
+                    stop=True,
+                )
+
+        def tanh(k, h):
+            nc.scalar.activation(
+                out=tts[k][:, 2 * h : 2 * h + 2, :].rearrange("p t (a l u) -> p (t a) l u", l=4, u=8),
+                in_=s1s[(k, h)][:].rearrange("p t (a u l) -> p (t a) l u", l=4, u=8),
+                func=ACT.Tanh,
+            )
+
+        hgs = {}
+        hqs = {}
+
+        def apply_gain(eng, k):
+            hg = keep.tile([P, 256, 4], BF16, tag="hg", bufs=PAIRS, align_bytes=64)
+            (nc.vector if eng == "V" else nc.gpsimd).tensor_tensor(
+                out=hg[:].rearrange("p (c i) t -> p c t i", i=4),
+                in0=tts[k][:].rearrange("p t (c i) -> p c t i", i=4),
+                in1=gain[:].unsqueeze(1).unsqueeze(3).to_broadcast([P, 64, 4, 4]),
+                op=ALU.mult,
+            )
+            hgs[k] = hg
+
+        def quantize_h(k):
+            hc = keep.tile([P, 256], I32, tag="hc", bufs=PAIRS, align_bytes=64)
+            hs = keep.tile([P, 256], U8, tag="hs", bufs=PAIRS, align_bytes=64)
+            nc.vector.quantize_mx(
+                out=hc[:].bitcast(FP8X4), scales=hs[:], in_=hgs[k][:].rearrange("p n t -> p (n t)")
+            )
+            hqs[k] = (hc, hs)
+
+        batches = [[0,10],[10,16]]
+        batch_of = [0,0,0,0,0,0,0,0,0,0,1,1,1,1,1,1]
+        zbs = {}
+
+        def blank(b):
+            i = batch_of[b]
+            if b == batches[i][0]:
+                zb = psum.tile([P, B], F32, tag="zb" if i == 0 else "s1", bufs=1 if i == 0 else 4)
+                zbs[i] = zb
+            k, c = b // 2, b % 2
+            col = b - batches[i][0]
+            for t in range(4):
+                nc.tensor.matmul(
+                    out=zbs[i][:, col : col + 1],
+                    lhsT=tts[k][:, t, c * 128 : (c + 1) * 128],
+                    rhs=wbf[:, t : t + 1],
+                    start=(t == 0),
+                    stop=(t == 3),
+                )
+
+        nm = keep.tile([P, B], F32)
+        ssum = keep.tile([P, B], F32)
+        lgs = {}
+        ots = {}
+
+        def logits(b):
+            hc, hs = hqs[b // 2]
+            c = b % 2
+            cols = slice(c * 128, (c + 1) * 128)
+            lg = psum.tile([P, V], F32, tag="lg", bufs=3)
+            nc.tensor.matmul_mx(
+                out=lg[:],
+                lhsT=hc[:, cols].bitcast(FP8X4),
+                lhsT_scale=hs[:, cols],
+                rhs=wo_c[:].bitcast(FP8X4),
+                rhs_scale=wo_s[:],
+                start=True,
+                stop=True,
+            )
+            lgs[b] = lg
+            if c == 0:
+                ot = keep.tile([P, 2, V], F32, tag="ot", bufs=PAIRS, align_bytes=64)
+                ots[b // 2] = ot
+
+        def evacuate(b):
+            nc.vector.tensor_scalar(
+                out=ots[b // 2][:, b % 2, :],
+                in0=lgs[b][:],
+                scalar1=-1.0,
+                scalar2=None,
+                op0=ALU.mult,
+                op1=ALU.min,
+                accum_out=nm[:, b : b + 1],
+            )
+
+        def exps(b):
+            junk = work.tile([P, V], F32)
+            nc.scalar.activation(
+                out=junk[:],
+                in_=ots[b // 2][:, b % 2, :],
+                func=ACT.Exp,
+                bias=nm[:, b : b + 1],
+                scale=-1.0,
+                accum_out=ssum[:, b : b + 1],
+            )
+
+        small = {}
+        for i in range(len(batches)):
+            for what in ("az", "ez", "e1", "mr", "qq", "ln", "ng", "y0", "ex", "aa", "uu", "vv", "ww", "y1"):
+                piece = keep.tile([P, B], F32, tag="%s%d" % (what, i), align_bytes=64)
+                small[(what, i)] = piece
+
+        engines = {"V": nc.vector, "G": nc.gpsimd}
+
+        def cols_of(i):
+            return slice(batches[i][0], batches[i][1])
+
+        def op_az(i):
+            w = batches[i][1] - batches[i][0]
+            nc.scalar.activation(out=small[("az", i)][:, cols_of(i)], in_=zbs[i][:, 0:w], func=ACT.Abs)
+
+        def op_ez(i):
+            nc.scalar.activation(out=small[("ez", i)][:, cols_of(i)], in_=small[("az", i)][:, cols_of(i)], func=ACT.Exp, scale=-1.0)
+
+        def op_mr(i):
+            w = batches[i][1] - batches[i][0]
+            nc.vector.scalar_tensor_tensor(
+                out=small[("mr", i)][:, cols_of(i)], in0=zbs[i][:, 0:w], scalar=0.0, in1=nm[:, cols_of(i)], op0=ALU.max, op1=ALU.subtract
+            )
+
+        def op_e1(eng, i):
+            engines[eng].tensor_scalar(
+                out=small[("e1", i)][:, cols_of(i)], in0=small[("ez", i)][:, cols_of(i)], scalar1=1.0, scalar2=1.0, op0=ALU.mult, op1=ALU.add
+            )
+
+        def op_bq(eng, i):
+            c = cols_of(i)
+            if eng == "V":
+                nc.vector.scalar_tensor_tensor(
+                    out=small[("qq", i)][:, c], in0=small[("ez", i)][:, c], scalar=1.0, in1=ssum[:, c], op0=ALU.add, op1=ALU.mult
+                )
+            else:
+                nc.gpsimd.tensor_tensor(out=small[("qq", i)][:, c], in0=small[("e1", i)][:, c], in1=ssum[:, c], op=ALU.mult)
+
+        def op_ln(i):
+            c = cols_of(i)
+            if batches[i][1] - batches[i][0] == 1:
+                nc.scalar.activation(out=small[("ln", i)][:, c], in_=ssum[:, c], func=ACT.Ln, scale=small[("e1", i)][:, c])
+            else:
+                nc.scalar.activation(out=small[("ln", i)][:, c], in_=small[("qq", i)][:, c], func=ACT.Ln)
+
+        def op_y0(i):
+            c = cols_of(i)
+            nc.vector.tensor_scalar(
+                out=small[("y0", i)][:, c],
+                in0=small[("qq", i)][:].bitcast(I32)[:, c],
+                scalar1=LN2 / 2.0**23,
+                scalar2=-LN2 * (127.0 - 0.0430) - 1.0,
+                op0=ALU.mult,
+                op1=ALU.add,
+            )
+
+        def op_nx(i, step):
+            c = cols_of(i)
+            y = small[("y0" if step == 1 else "y1", i)][:, c]
+            nc.scalar.activation(out=small[("ex", i)][:, c], in_=y, func=ACT.Exp, bias=minus_one[:], scale=-1.0)
+
+        def op_na(eng, i, step):
+            c = cols_of(i)
+            s = lambda what: small[(what, i)][:, c]
+            if eng == "V":
+                if step == 0:
+                    nc.vector.tensor_tensor(out=s("aa"), in0=s("ex"), in1=s("qq"), op=ALU.mult)
+                elif step == 1:
+                    nc.vector.tensor_scalar(
+                        out=s("uu"), in0=s("aa"), scalar1=-0.5, scalar2=1.5, op0=ALU.mult, op1=ALU.add
+                    )
+                elif step == 2:
+                    nc.vector.scalar_tensor_tensor(
+                        out=s("ww"), in0=s("aa"), scalar=-1.0, in1=s("uu"), op0=ALU.add, op1=ALU.mult
+                    )
+                else:
+                    nc.vector.tensor_tensor(out=s("y1"), in0=s("y0"), in1=s("ww"), op=ALU.add)
+            else:
+                if step == 0:
+                    nc.gpsimd.tensor_tensor(out=s("aa"), in0=s("ex"), in1=s("qq"), op=ALU.mult)
+                elif step == 1:
+                    nc.gpsimd.tensor_scalar(
+                        out=s("uu"), in0=s("aa"), scalar1=-0.5, scalar2=1.5, op0=ALU.mult, op1=ALU.add
+                    )
+                elif step == 2:
+                    nc.gpsimd.tensor_scalar(
+                        out=s("vv"), in0=s("aa"), scalar1=1.0, scalar2=-1.0, op0=ALU.mult, op1=ALU.add
+                    )
+                elif step == 3:
+                    nc.gpsimd.tensor_tensor(out=s("ww"), in0=s("vv"), in1=s("uu"), op=ALU.mult)
+                else:
+                    nc.gpsimd.tensor_tensor(out=s("y1"), in0=s("y0"), in1=s("ww"), op=ALU.add)
+
+        def op_nb(eng, i, step):
+            c = cols_of(i)
+            s = lambda what: small[(what, i)][:, c]
+            if step == 0:
+                engines[eng].tensor_tensor(out=s("vv" if eng == "V" else "aa"), in0=s("ex"), in1=s("qq"), op=ALU.mult)
+            else:
+                engines[eng].tensor_tensor(
+                    out=s("ln"), in0=s("y1"), in1=s("vv" if eng == "V" else "aa"), op=ALU.add
+                )
+
+        def op_ng(eng, i):
+            c = cols_of(i)
+            if eng == "V":
+                nc.vector.scalar_tensor_tensor(
+                    out=small[("ng", i)][:, c], in0=small[("ln", i)][:, c], scalar=-1.0, in1=small[("mr", i)][:, c], op0=ALU.mult, op1=ALU.subtract
+                )
+            else:
+                nc.gpsimd.tensor_tensor(out=small[("ng", i)][:, c], in0=small[("ln", i)][:, c], in1=small[("mr", i)][:, c], op=ALU.add)
+
+        beng = "GVGVGG"
+
+        def finish(eng, b):
+            o = ots[b // 2][:, b % 2, :]
+            n = small[("ng", batch_of[b])][:, b : b + 1]
+            negated = beng[batch_of[b]] == "V"
+            if eng == "S":
+                nc.scalar.activation(out=o, in_=o, func=ACT.Identity, bias=n, scale=-1.0)
+            elif negated:
+                engines[eng].tensor_scalar(out=o, in0=o, scalar1=-1.0, scalar2=n, op0=ALU.mult, op1=ALU.add)
+            else:
+                engines[eng].tensor_scalar(out=o, in0=o, scalar1=n, scalar2=-1.0, op0=ALU.add, op1=ALU.mult)
+
+        rows = out.rearrange("b i u v -> (b i u) v").rearrange("(k c p) v -> k p c v", c=2, p=P)
+
+        def store(b):
+            nc.sync.dma_start(out=rows[b // 2][:, b % 2, :], in_=ots[b // 2][:, b % 2, :])
+
+        def il_w(eng, which, h):
+            if which == "wo":
+                copy(
+                    eng,
+                    wo_g[:, h * 1024 : (h + 1) * 1024].rearrange("p (n j) -> p n j", j=4),
+                    wo_raw[:, :, h * 256 : (h + 1) * 256].rearrange("p j n -> p n j"),
+                )
+            elif which == "we":
+                copy(eng, half_grouped(we_g, h), half_raw(we_raw, h))
+            else:
+                copy(eng, half_grouped(wp_g, h), half_raw(wp_w, h))
+
+        widen("V", 0)
+        widen("S", 3)
+        transpose_pred()
+        widen("V", 1)
+        widen("V", 2)
+        copy_pred("S")
+        transpose_enc()
+        il_w("V", "wp", 0)
+        copy_enc("S")
+        il_w("V", "we", 0)
+        il_w("S", "we", 1)
+        nc.vector.quantize_mx(out=pred_c[:].bitcast(FP8X4), scales=pred_s[:], in_=pred_g[:])
+        nc.vector.quantize_mx(out=enc_c[:].bitcast(FP8X4), scales=enc_s[:], in_=enc_g[:])
+        quantize_half(wp_g, wp_c, wp_s, 0)
+        il_w("S", "wp", 1)
+        replicate(2, 2)
+        quantize_half(we_g, we_c, we_s, 0)
+        replicate(0, 2)
+        first_stage(1, 0)
+        il_w("S", "wo", 1)
+        quantize_half(we_g, we_c, we_s, 1)
+        quantize_half(wp_g, wp_c, wp_s, 1)
+        first_stage(0, 0)
+        replicate(4, 4)
+        first_stage(0, 1)
+        tanh(0, 0)
+        replicate(8, 8)
+        first_stage(1, 1)
+        tanh(0, 1)
+        first_stage(2, 0)
+        tanh(1, 0)
+        first_stage(2, 1)
+        il_w("V", "wo", 0)
+        tanh(1, 1)
+        blank(0)
+        tanh(2, 0)
+        quantize_half(wo_g, wo_c, wo_s, 1)
+        first_stage(3, 0)
+        quantize_half(wo_g, wo_c, wo_s, 0)
+        tanh(2, 1)
+        apply_gain("V", 0)
+        first_stage(3, 1)
+        tanh(3, 0)
+        first_stage(4, 0)
+        tanh(3, 1)
+        apply_gain("V", 1)
+        first_stage(4, 1)
+        tanh(4, 0)
+        first_stage(5, 0)
+        tanh(4, 1)
+        quantize_h(0)
+        first_stage(5, 1)
+        quantize_h(1)
+        tanh(5, 0)
+        apply_gain("V", 3)
+        logits(0)
+        logits(1)
+        tanh(5, 1)
+        logits(2)
+        blank(1)
+        apply_gain("G", 2)
+        evacuate(0)
+        first_stage(6, 0)
+        evacuate(1)
+        exps(0)
+        logits(3)
+        evacuate(2)
+        first_stage(6, 1)
+        tanh(6, 0)
+        blank(2)
+        evacuate(3)
+        exps(1)
+        quantize_h(2)
+        blank(3)
+        tanh(6, 1)
+        quantize_h(3)
+        apply_gain("V", 4)
+        logits(4)
+        exps(2)
+        logits(5)
+        logits(6)
+        exps(3)
+        first_stage(7, 0)
+        evacuate(4)
+        first_stage(7, 1)
+        tanh(7, 0)
+        evacuate(5)
+        blank(4)
+        tanh(7, 1)
+        quantize_h(4)
+        logits(7)
+        evacuate(6)
+        exps(4)
+        blank(5)
+        apply_gain("G", 7)
+        evacuate(7)
+        exps(5)
+        logits(8)
+        logits(9)
+        exps(6)
+        evacuate(8)
+        blank(6)
+        exps(7)
+        evacuate(9)
+        blank(7)
+        exps(8)
+        apply_gain("V", 5)
+        blank(8)
+        exps(9)
+        blank(9)
+        apply_gain("V", 6)
+        blank(10)
+        op_az(0)
+        op_ez(0)
+        blank(11)
+        quantize_h(5)
+        op_mr(0)
+        op_e1("G", 0)
+        quantize_h(6)
+        blank(12)
+        quantize_h(7)
+        op_bq("G", 0)
+        logits(10)
+        logits(11)
+        op_ln(0)
+        evacuate(10)
+        logits(12)
+        op_ng("G", 0)
+        blank(13)
+        finish("G", 0)
+        store(0)
+        evacuate(11)
+        logits(13)
+        finish("G", 2)
+        store(2)
+        blank(14)
+        evacuate(12)
+        exps(10)
+        finish("G", 3)
+        store(3)
+        evacuate(13)
+        logits(14)
+        logits(15)
+        exps(11)
+        finish("G", 4)
+        store(4)
+        blank(15)
+        evacuate(14)
+        exps(12)
+        finish("G", 5)
+        store(5)
+        evacuate(15)
+        op_az(1)
+        exps(13)
+        finish("G", 6)
+        store(6)
+        op_mr(1)
+        op_ez(1)
+        finish("V", 1)
+        store(1)
+        exps(14)
+        finish("V", 8)
+        store(8)
+        finish("V", 9)
+        store(9)
+        exps(15)
+        finish("G", 7)
+        store(7)
+        op_bq("V", 1)
+        op_ln(1)
+        op_ng("V", 1)
+        finish("V", 10)
+        store(10)
+        finish("S", 12)
+        store(12)
+        finish("V", 13)
+        store(13)
+        finish("V", 14)
+        store(14)
+        finish("G", 11)
+        store(11)
+        finish("G", 15)
+        store(15)

@@ -13,7 +13,6 @@ ALU = mybir.AluOpType
 ACT = mybir.ActivationFunctionType
 
 P = 128
-LN2 = 0.6931471805599453
 B, T, U, K, J, V = 16, 16, 8, 512, 512, 512
 ROWS = B * T * U
 PAIRS = B // 2
@@ -53,8 +52,8 @@ def tile_hybridautoregressivetransducerjoiner_kernel(
         nc.vector.memset(warm[:], 0.0)
         warm_out = keep.tile([P, 1], F32)
         nc.scalar.activation(out=warm_out[:], in_=warm[:], func=ACT.Exp)
-        minus_one = keep.tile([P, 1], F32)
-        nc.gpsimd.memset(minus_one[:], -1.0)
+        ones = keep.tile([P, 1], F32)
+        nc.gpsimd.memset(ones[:], 1.0)
         ident = keep.tile([P, P], F32)
         make_identity(nc, ident[:])
         enc_s = keep.tile([P, B * T], U8, align_bytes=64)
@@ -239,24 +238,48 @@ def tile_hybridautoregressivetransducerjoiner_kernel(
             )
             hqs[k] = (hc, hs)
 
-        batches = [[0,10],[10,16]]
-        batch_of = [0,0,0,0,0,0,0,0,0,0,1,1,1,1,1,1]
+        batches = [[0,11],[11,16]]
+        batch_of = [0,0,0,0,0,0,0,0,0,0,0,1,1,1,1,1]
         zbs = {}
+
+        zmode = "PSPSVPSP"
+        zsum = {}
+
+        def presum(eng, k, step):
+            if step == 0:
+                zr = keep.tile([P, 256], F32, tag="zr%d" % k, align_bytes=64)
+                zsum[k] = zr
+            z = zsum[k][:]
+            x = tts[k][:, step, :]
+            w = wbf[:, step : step + 1]
+            if step == 0:
+                if eng == "S":
+                    nc.scalar.activation(out=z, in_=x, func=ACT.Copy, scale=w)
+                else:
+                    nc.vector.tensor_scalar(out=z, in0=x, scalar1=w, scalar2=None, op0=ALU.mult)
+            else:
+                nc.vector.scalar_tensor_tensor(out=z, in0=x, scalar=w, in1=z, op0=ALU.mult, op1=ALU.add)
 
         def blank(b):
             i = batch_of[b]
-            if b == batches[i][0]:
+            if i not in zbs:
                 zb = psum.tile([P, B], F32, tag="zb" if i == 0 else "s1", bufs=1 if i == 0 else 4)
                 zbs[i] = zb
             k, c = b // 2, b % 2
             col = b - batches[i][0]
-            for t in range(4):
+            cols = slice(c * 128, (c + 1) * 128)
+            if zmode[k] == "P":
+                for t in range(4):
+                    nc.tensor.matmul(
+                        out=zbs[i][:, col : col + 1],
+                        lhsT=tts[k][:, t, cols],
+                        rhs=wbf[:, t : t + 1],
+                        start=(t == 0),
+                        stop=(t == 3),
+                    )
+            else:
                 nc.tensor.matmul(
-                    out=zbs[i][:, col : col + 1],
-                    lhsT=tts[k][:, t, c * 128 : (c + 1) * 128],
-                    rhs=wbf[:, t : t + 1],
-                    start=(t == 0),
-                    stop=(t == 3),
+                    out=zbs[i][:, col : col + 1], lhsT=zsum[k][:, cols], rhs=ones[:], start=True, stop=True
                 )
 
         nm = keep.tile([P, B], F32)
@@ -307,7 +330,7 @@ def tile_hybridautoregressivetransducerjoiner_kernel(
 
         small = {}
         for i in range(len(batches)):
-            for what in ("az", "ez", "e1", "mr", "qq", "ln", "ng", "y0", "ex", "aa", "uu", "vv", "ww", "y1"):
+            for what in ("az", "ez", "e1", "mr", "qq", "ln", "ng"):
                 piece = keep.tile([P, B], F32, tag="%s%d" % (what, i), align_bytes=64)
                 small[(what, i)] = piece
 
@@ -350,64 +373,6 @@ def tile_hybridautoregressivetransducerjoiner_kernel(
             else:
                 nc.scalar.activation(out=small[("ln", i)][:, c], in_=small[("qq", i)][:, c], func=ACT.Ln)
 
-        def op_y0(i):
-            c = cols_of(i)
-            nc.vector.tensor_scalar(
-                out=small[("y0", i)][:, c],
-                in0=small[("qq", i)][:].bitcast(I32)[:, c],
-                scalar1=LN2 / 2.0**23,
-                scalar2=-LN2 * (127.0 - 0.0430) - 1.0,
-                op0=ALU.mult,
-                op1=ALU.add,
-            )
-
-        def op_nx(i, step):
-            c = cols_of(i)
-            y = small[("y0" if step == 1 else "y1", i)][:, c]
-            nc.scalar.activation(out=small[("ex", i)][:, c], in_=y, func=ACT.Exp, bias=minus_one[:], scale=-1.0)
-
-        def op_na(eng, i, step):
-            c = cols_of(i)
-            s = lambda what: small[(what, i)][:, c]
-            if eng == "V":
-                if step == 0:
-                    nc.vector.tensor_tensor(out=s("aa"), in0=s("ex"), in1=s("qq"), op=ALU.mult)
-                elif step == 1:
-                    nc.vector.tensor_scalar(
-                        out=s("uu"), in0=s("aa"), scalar1=-0.5, scalar2=1.5, op0=ALU.mult, op1=ALU.add
-                    )
-                elif step == 2:
-                    nc.vector.scalar_tensor_tensor(
-                        out=s("ww"), in0=s("aa"), scalar=-1.0, in1=s("uu"), op0=ALU.add, op1=ALU.mult
-                    )
-                else:
-                    nc.vector.tensor_tensor(out=s("y1"), in0=s("y0"), in1=s("ww"), op=ALU.add)
-            else:
-                if step == 0:
-                    nc.gpsimd.tensor_tensor(out=s("aa"), in0=s("ex"), in1=s("qq"), op=ALU.mult)
-                elif step == 1:
-                    nc.gpsimd.tensor_scalar(
-                        out=s("uu"), in0=s("aa"), scalar1=-0.5, scalar2=1.5, op0=ALU.mult, op1=ALU.add
-                    )
-                elif step == 2:
-                    nc.gpsimd.tensor_scalar(
-                        out=s("vv"), in0=s("aa"), scalar1=1.0, scalar2=-1.0, op0=ALU.mult, op1=ALU.add
-                    )
-                elif step == 3:
-                    nc.gpsimd.tensor_tensor(out=s("ww"), in0=s("vv"), in1=s("uu"), op=ALU.mult)
-                else:
-                    nc.gpsimd.tensor_tensor(out=s("y1"), in0=s("y0"), in1=s("ww"), op=ALU.add)
-
-        def op_nb(eng, i, step):
-            c = cols_of(i)
-            s = lambda what: small[(what, i)][:, c]
-            if step == 0:
-                engines[eng].tensor_tensor(out=s("vv" if eng == "V" else "aa"), in0=s("ex"), in1=s("qq"), op=ALU.mult)
-            else:
-                engines[eng].tensor_tensor(
-                    out=s("ln"), in0=s("y1"), in1=s("vv" if eng == "V" else "aa"), op=ALU.add
-                )
-
         def op_ng(eng, i):
             c = cols_of(i)
             if eng == "V":
@@ -417,7 +382,7 @@ def tile_hybridautoregressivetransducerjoiner_kernel(
             else:
                 nc.gpsimd.tensor_tensor(out=small[("ng", i)][:, c], in0=small[("ln", i)][:, c], in1=small[("mr", i)][:, c], op=ALU.add)
 
-        beng = "GVGVGG"
+        beng = "GGGGGG"
 
         def finish(eng, b):
             o = ots[b // 2][:, b % 2, :]
@@ -452,181 +417,198 @@ def tile_hybridautoregressivetransducerjoiner_kernel(
         transpose_pred()
         widen("V", 1)
         widen("V", 2)
-        copy_pred("S")
         transpose_enc()
+        copy_pred("S")
         il_w("V", "wp", 0)
+        il_w("V", "wp", 1)
         copy_enc("S")
-        il_w("V", "we", 0)
-        il_w("S", "we", 1)
         nc.vector.quantize_mx(out=pred_c[:].bitcast(FP8X4), scales=pred_s[:], in_=pred_g[:])
+        il_w("S", "we", 0)
         nc.vector.quantize_mx(out=enc_c[:].bitcast(FP8X4), scales=enc_s[:], in_=enc_g[:])
         quantize_half(wp_g, wp_c, wp_s, 0)
-        il_w("S", "wp", 1)
-        replicate(2, 2)
+        replicate(2, 4)
+        il_w("S", "we", 1)
         quantize_half(we_g, we_c, we_s, 0)
         replicate(0, 2)
         first_stage(1, 0)
+        quantize_half(wp_g, wp_c, wp_s, 1)
         il_w("S", "wo", 1)
         quantize_half(we_g, we_c, we_s, 1)
-        quantize_half(wp_g, wp_c, wp_s, 1)
+        replicate(6, 4)
         first_stage(0, 0)
-        replicate(4, 4)
+        tanh(1, 0)
+        il_w("V", "wo", 0)
         first_stage(0, 1)
         tanh(0, 0)
-        replicate(8, 8)
         first_stage(1, 1)
-        tanh(0, 1)
-        first_stage(2, 0)
-        tanh(1, 0)
-        first_stage(2, 1)
-        il_w("V", "wo", 0)
-        tanh(1, 1)
-        blank(0)
-        tanh(2, 0)
         quantize_half(wo_g, wo_c, wo_s, 1)
-        first_stage(3, 0)
         quantize_half(wo_g, wo_c, wo_s, 0)
-        tanh(2, 1)
-        apply_gain("V", 0)
-        first_stage(3, 1)
+        tanh(0, 1)
+        first_stage(3, 0)
+        replicate(10, 6)
+        tanh(1, 1)
+        first_stage(2, 0)
         tanh(3, 0)
-        first_stage(4, 0)
-        tanh(3, 1)
+        first_stage(2, 1)
+        apply_gain("V", 0)
+        tanh(2, 0)
+        first_stage(3, 1)
+        tanh(2, 1)
+        blank(0)
         apply_gain("V", 1)
-        first_stage(4, 1)
-        tanh(4, 0)
-        first_stage(5, 0)
-        tanh(4, 1)
+        tanh(3, 1)
+        presum("S", 1, 0)
+        first_stage(4, 0)
+        presum("S", 3, 0)
         quantize_h(0)
-        first_stage(5, 1)
+        first_stage(4, 1)
+        presum("V", 1, 1)
+        tanh(4, 0)
         quantize_h(1)
-        tanh(5, 0)
-        apply_gain("V", 3)
         logits(0)
+        presum("V", 1, 2)
+        tanh(4, 1)
         logits(1)
-        tanh(5, 1)
+        apply_gain("V", 3)
         logits(2)
         blank(1)
         apply_gain("G", 2)
         evacuate(0)
-        first_stage(6, 0)
+        first_stage(5, 0)
         evacuate(1)
         exps(0)
         logits(3)
+        first_stage(5, 1)
         evacuate(2)
-        first_stage(6, 1)
-        tanh(6, 0)
-        blank(2)
+        tanh(5, 0)
+        first_stage(6, 0)
         evacuate(3)
-        exps(1)
+        tanh(5, 1)
+        first_stage(6, 1)
+        presum("V", 1, 3)
+        tanh(6, 0)
+        blank(4)
         quantize_h(2)
-        blank(3)
+        presum("V", 3, 1)
         tanh(6, 1)
         quantize_h(3)
-        apply_gain("V", 4)
+        exps(1)
+        presum("V", 3, 2)
+        blank(2)
+        presum("V", 4, 0)
         logits(4)
+        apply_gain("V", 4)
         exps(2)
+        blank(3)
         logits(5)
-        logits(6)
         exps(3)
-        first_stage(7, 0)
+        logits(6)
+        blank(5)
+        presum("V", 3, 3)
+        presum("S", 6, 0)
+        apply_gain("G", 5)
         evacuate(4)
-        first_stage(7, 1)
-        tanh(7, 0)
+        first_stage(7, 0)
         evacuate(5)
-        blank(4)
-        tanh(7, 1)
-        quantize_h(4)
+        exps(4)
         logits(7)
         evacuate(6)
-        exps(4)
-        blank(5)
-        apply_gain("G", 7)
+        first_stage(7, 1)
+        tanh(7, 0)
         evacuate(7)
-        exps(5)
-        logits(8)
-        logits(9)
-        exps(6)
-        evacuate(8)
         blank(6)
-        exps(7)
-        evacuate(9)
+        exps(5)
         blank(7)
-        exps(8)
-        apply_gain("V", 5)
-        blank(8)
-        exps(9)
-        blank(9)
-        apply_gain("V", 6)
         blank(10)
-        op_az(0)
-        op_ez(0)
-        blank(11)
+        presum("V", 4, 1)
+        tanh(7, 1)
+        quantize_h(4)
+        presum("V", 4, 2)
+        exps(6)
         quantize_h(5)
-        op_mr(0)
-        op_e1("G", 0)
-        quantize_h(6)
-        blank(12)
-        quantize_h(7)
-        op_bq("G", 0)
+        logits(8)
+        presum("V", 4, 3)
+        exps(7)
+        logits(9)
+        apply_gain("G", 7)
+        evacuate(8)
         logits(10)
-        logits(11)
-        op_ln(0)
+        blank(8)
+        blank(9)
+        evacuate(9)
+        blank(11)
+        exps(8)
         evacuate(10)
+        op_az(0)
+        exps(9)
+        logits(11)
+        op_mr(0)
+        blank(14)
+        exps(10)
+        apply_gain("V", 6)
+        op_ez(0)
+        blank(15)
+        presum("V", 6, 1)
+        evacuate(11)
+        op_e1("G", 0)
+        op_bq("G", 0)
+        presum("V", 6, 2)
+        op_ln(0)
+        quantize_h(6)
+        presum("V", 6, 3)
+        quantize_h(7)
         logits(12)
         op_ng("G", 0)
-        blank(13)
-        finish("G", 0)
-        store(0)
-        evacuate(11)
         logits(13)
-        finish("G", 2)
-        store(2)
-        blank(14)
-        evacuate(12)
-        exps(10)
-        finish("G", 3)
-        store(3)
-        evacuate(13)
-        logits(14)
-        logits(15)
-        exps(11)
-        finish("G", 4)
-        store(4)
-        blank(15)
-        evacuate(14)
-        exps(12)
-        finish("G", 5)
-        store(5)
-        evacuate(15)
-        op_az(1)
-        exps(13)
-        finish("G", 6)
-        store(6)
-        op_mr(1)
-        op_ez(1)
         finish("V", 1)
         store(1)
+        evacuate(12)
+        finish("G", 0)
+        store(0)
+        exps(11)
+        blank(12)
+        logits(14)
+        finish("G", 2)
+        store(2)
+        evacuate(13)
+        blank(13)
+        exps(12)
+        logits(15)
+        finish("G", 5)
+        store(5)
+        evacuate(14)
+        op_az(1)
+        exps(13)
+        finish("G", 10)
+        store(10)
+        evacuate(15)
         exps(14)
+        finish("V", 3)
+        store(3)
+        exps(15)
+        finish("V", 4)
+        store(4)
+        finish("V", 6)
+        store(6)
+        finish("V", 7)
+        store(7)
+        op_ez(1)
         finish("V", 8)
         store(8)
         finish("V", 9)
         store(9)
-        exps(15)
-        finish("G", 7)
-        store(7)
-        op_bq("V", 1)
+        op_mr(1)
+        op_e1("G", 1)
+        op_bq("G", 1)
         op_ln(1)
-        op_ng("V", 1)
-        finish("V", 10)
-        store(10)
-        finish("S", 12)
-        store(12)
+        op_ng("G", 1)
         finish("V", 13)
         store(13)
-        finish("V", 14)
-        store(14)
+        finish("V", 15)
+        store(15)
         finish("G", 11)
         store(11)
-        finish("G", 15)
-        store(15)
+        finish("G", 12)
+        store(12)
+        finish("G", 14)
+        store(14)

@@ -13,6 +13,8 @@ ALU = mybir.AluOpType
 ACT = mybir.ActivationFunctionType
 
 P = 128
+ZN = 32
+ZNB = 10
 B, T, U, K, J, V = 16, 16, 8, 512, 512, 512
 ROWS = B * T * U
 PAIRS = B // 2
@@ -64,6 +66,8 @@ def tile_hybridautoregressivetransducerjoiner_kernel(
         nc.gpsimd.tensor_copy(out=gain[:], in_=gj_raw[:])
         wbf = keep.tile([P, 4], F32)
         nc.gpsimd.tensor_copy(out=wbf[:], in_=wb_raw[:])
+        wbr = keep.tile([P, 4, ZN], F32)
+        nc.gpsimd.tensor_copy(out=wbr[:], in_=wbf[:].unsqueeze(2).to_broadcast([P, 4, ZN]))
 
         enc_g = keep.tile([P, B * T * 4], BF16, align_bytes=64)
         pred_g = keep.tile([P, B * U * 16], BF16, align_bytes=64)
@@ -238,11 +242,11 @@ def tile_hybridautoregressivetransducerjoiner_kernel(
             )
             hqs[k] = (hc, hs)
 
-        batches = [[0,11],[11,16]]
-        batch_of = [0,0,0,0,0,0,0,0,0,0,0,1,1,1,1,1]
+        batches = [[0,10],[10,16]]
+        batch_of = [0,0,0,0,0,0,0,0,0,0,1,1,1,1,1,1]
         zbs = {}
 
-        zmode = "PSPSVPSP"
+        zmode = "PVSSPPPS"
         zsum = {}
 
         def presum(eng, k, step):
@@ -263,23 +267,24 @@ def tile_hybridautoregressivetransducerjoiner_kernel(
         def blank(b):
             i = batch_of[b]
             if i not in zbs:
-                zb = psum.tile([P, B], F32, tag="zb" if i == 0 else "s1", bufs=1 if i == 0 else 4)
+                zb = psum.tile([P, batches[i][1] - batches[i][0], ZN], F32, tag="zb" if i == 0 else "s1", bufs=1 if i == 0 else 4)
                 zbs[i] = zb
             k, c = b // 2, b % 2
             col = b - batches[i][0]
             cols = slice(c * 128, (c + 1) * 128)
+            n = ZN if b >= ZNB else 1
             if zmode[k] == "P":
                 for t in range(4):
                     nc.tensor.matmul(
-                        out=zbs[i][:, col : col + 1],
+                        out=zbs[i][:, col, 0:n],
                         lhsT=tts[k][:, t, cols],
-                        rhs=wbf[:, t : t + 1],
+                        rhs=wbr[:, t, 0:n],
                         start=(t == 0),
                         stop=(t == 3),
                     )
             else:
                 nc.tensor.matmul(
-                    out=zbs[i][:, col : col + 1], lhsT=zsum[k][:, cols], rhs=ones[:], start=True, stop=True
+                    out=zbs[i][:, col, 0:1], lhsT=zsum[k][:, cols], rhs=ones[:], start=True, stop=True
                 )
 
         nm = keep.tile([P, B], F32)
@@ -340,16 +345,14 @@ def tile_hybridautoregressivetransducerjoiner_kernel(
             return slice(batches[i][0], batches[i][1])
 
         def op_az(i):
-            w = batches[i][1] - batches[i][0]
-            nc.scalar.activation(out=small[("az", i)][:, cols_of(i)], in_=zbs[i][:, 0:w], func=ACT.Abs)
+            nc.scalar.activation(out=small[("az", i)][:, cols_of(i)], in_=zbs[i][:, :, 0], func=ACT.Abs)
 
         def op_ez(i):
             nc.scalar.activation(out=small[("ez", i)][:, cols_of(i)], in_=small[("az", i)][:, cols_of(i)], func=ACT.Exp, scale=-1.0)
 
         def op_mr(i):
-            w = batches[i][1] - batches[i][0]
             nc.vector.scalar_tensor_tensor(
-                out=small[("mr", i)][:, cols_of(i)], in0=zbs[i][:, 0:w], scalar=0.0, in1=nm[:, cols_of(i)], op0=ALU.max, op1=ALU.subtract
+                out=small[("mr", i)][:, cols_of(i)], in0=zbs[i][:, :, 0], scalar=0.0, in1=nm[:, cols_of(i)], op0=ALU.max, op1=ALU.subtract
             )
 
         def op_e1(eng, i):
@@ -382,7 +385,7 @@ def tile_hybridautoregressivetransducerjoiner_kernel(
             else:
                 nc.gpsimd.tensor_tensor(out=small[("ng", i)][:, c], in0=small[("ln", i)][:, c], in1=small[("mr", i)][:, c], op=ALU.add)
 
-        beng = "GGGGGG"
+        beng = "GVVVVG"
 
         def finish(eng, b):
             o = ots[b // 2][:, b % 2, :]
@@ -404,8 +407,8 @@ def tile_hybridautoregressivetransducerjoiner_kernel(
             if which == "wo":
                 copy(
                     eng,
-                    wo_g[:, h * 1024 : (h + 1) * 1024].rearrange("p (n j) -> p n j", j=4),
-                    wo_raw[:, :, h * 256 : (h + 1) * 256].rearrange("p j n -> p n j"),
+                    wo_g[:, h * 1024 : (h + 1) * 1024].rearrange("p (c i j) -> p c j i", i=4, j=4),
+                    wo_raw[:, :, h * 256 : (h + 1) * 256].rearrange("p j (c i) -> p c j i", i=4),
                 )
             elif which == "we":
                 copy(eng, half_grouped(we_g, h), half_raw(we_raw, h))
@@ -413,202 +416,200 @@ def tile_hybridautoregressivetransducerjoiner_kernel(
                 copy(eng, half_grouped(wp_g, h), half_raw(wp_w, h))
 
         widen("V", 0)
-        widen("S", 3)
+        widen("S", 1)
         transpose_pred()
-        widen("V", 1)
         widen("V", 2)
+        widen("V", 3)
         transpose_enc()
-        copy_pred("S")
-        il_w("V", "wp", 0)
-        il_w("V", "wp", 1)
-        copy_enc("S")
-        nc.vector.quantize_mx(out=pred_c[:].bitcast(FP8X4), scales=pred_s[:], in_=pred_g[:])
+        copy_pred("V")
+        il_w("S", "wp", 0)
+        copy_enc("V")
         il_w("S", "we", 0)
+        nc.vector.quantize_mx(out=pred_c[:].bitcast(FP8X4), scales=pred_s[:], in_=pred_g[:])
         nc.vector.quantize_mx(out=enc_c[:].bitcast(FP8X4), scales=enc_s[:], in_=enc_g[:])
         quantize_half(wp_g, wp_c, wp_s, 0)
-        replicate(2, 4)
-        il_w("S", "we", 1)
+        il_w("S", "wp", 1)
+        il_w("V", "we", 1)
         quantize_half(we_g, we_c, we_s, 0)
         replicate(0, 2)
-        first_stage(1, 0)
-        quantize_half(wp_g, wp_c, wp_s, 1)
-        il_w("S", "wo", 1)
+        il_w("S", "wo", 0)
         quantize_half(we_g, we_c, we_s, 1)
-        replicate(6, 4)
+        quantize_half(wp_g, wp_c, wp_s, 1)
         first_stage(0, 0)
-        tanh(1, 0)
-        il_w("V", "wo", 0)
+        replicate(2, 4)
+        il_w("S", "wo", 1)
+        quantize_half(wo_g, wo_c, wo_s, 0)
         first_stage(0, 1)
+        replicate(6, 10)
+        first_stage(1, 0)
         tanh(0, 0)
         first_stage(1, 1)
-        quantize_half(wo_g, wo_c, wo_s, 1)
-        quantize_half(wo_g, wo_c, wo_s, 0)
         tanh(0, 1)
-        first_stage(3, 0)
-        replicate(10, 6)
-        tanh(1, 1)
         first_stage(2, 0)
-        tanh(3, 0)
+        tanh(1, 0)
+        quantize_half(wo_g, wo_c, wo_s, 1)
         first_stage(2, 1)
         apply_gain("V", 0)
+        tanh(1, 1)
+        first_stage(3, 0)
         tanh(2, 0)
         first_stage(3, 1)
         tanh(2, 1)
-        blank(0)
+        presum("V", 1, 0)
         apply_gain("V", 1)
+        blank(0)
+        tanh(3, 0)
         tanh(3, 1)
-        presum("S", 1, 0)
         first_stage(4, 0)
-        presum("S", 3, 0)
         quantize_h(0)
-        first_stage(4, 1)
+        presum("S", 2, 0)
         presum("V", 1, 1)
-        tanh(4, 0)
+        presum("S", 3, 0)
+        first_stage(4, 1)
         quantize_h(1)
+        tanh(4, 0)
+        apply_gain("V", 2)
         logits(0)
-        presum("V", 1, 2)
-        tanh(4, 1)
         logits(1)
-        apply_gain("V", 3)
+        tanh(4, 1)
         logits(2)
-        blank(1)
-        apply_gain("G", 2)
-        evacuate(0)
         first_stage(5, 0)
+        presum("V", 1, 2)
+        first_stage(5, 1)
+        presum("V", 2, 1)
+        tanh(5, 0)
+        quantize_h(2)
+        first_stage(6, 0)
+        presum("V", 1, 3)
+        tanh(5, 1)
+        presum("V", 2, 2)
+        first_stage(6, 1)
+        presum("V", 3, 1)
+        tanh(6, 0)
+        blank(1)
+        apply_gain("G", 3)
+        evacuate(0)
+        tanh(6, 1)
         evacuate(1)
         exps(0)
         logits(3)
-        first_stage(5, 1)
         evacuate(2)
-        tanh(5, 0)
-        first_stage(6, 0)
-        evacuate(3)
-        tanh(5, 1)
-        first_stage(6, 1)
-        presum("V", 1, 3)
-        tanh(6, 0)
-        blank(4)
-        quantize_h(2)
-        presum("V", 3, 1)
-        tanh(6, 1)
-        quantize_h(3)
-        exps(1)
-        presum("V", 3, 2)
-        blank(2)
-        presum("V", 4, 0)
-        logits(4)
-        apply_gain("V", 4)
-        exps(2)
-        blank(3)
-        logits(5)
-        exps(3)
-        logits(6)
-        blank(5)
-        presum("V", 3, 3)
-        presum("S", 6, 0)
-        apply_gain("G", 5)
-        evacuate(4)
         first_stage(7, 0)
-        evacuate(5)
-        exps(4)
-        logits(7)
-        evacuate(6)
+        exps(1)
+        evacuate(3)
+        logits(4)
+        apply_gain("G", 4)
+        exps(2)
+        logits(5)
         first_stage(7, 1)
+        evacuate(4)
         tanh(7, 0)
+        blank(2)
+        evacuate(5)
+        exps(3)
+        blank(3)
+        blank(8)
+        tanh(7, 1)
+        presum("V", 2, 3)
+        exps(4)
+        presum("V", 3, 2)
+        blank(9)
+        quantize_h(3)
+        exps(5)
+        quantize_h(4)
+        presum("V", 3, 3)
+        presum("S", 7, 0)
+        apply_gain("V", 5)
+        logits(6)
+        logits(7)
+        logits(8)
+        apply_gain("G", 6)
+        evacuate(6)
+        blank(4)
+        blank(5)
         evacuate(7)
         blank(6)
-        exps(5)
-        blank(7)
-        blank(10)
-        presum("V", 4, 1)
-        tanh(7, 1)
-        quantize_h(4)
-        presum("V", 4, 2)
         exps(6)
-        quantize_h(5)
-        logits(8)
-        presum("V", 4, 3)
-        exps(7)
         logits(9)
-        apply_gain("G", 7)
         evacuate(8)
-        logits(10)
-        blank(8)
-        blank(9)
+        blank(7)
+        exps(7)
+        blank(10)
         evacuate(9)
-        blank(11)
-        exps(8)
-        evacuate(10)
         op_az(0)
-        exps(9)
-        logits(11)
-        op_mr(0)
-        blank(14)
-        exps(10)
-        apply_gain("V", 6)
+        exps(8)
+        quantize_h(5)
+        quantize_h(6)
         op_ez(0)
-        blank(15)
-        presum("V", 6, 1)
-        evacuate(11)
+        exps(9)
+        op_mr(0)
+        apply_gain("V", 7)
+        logits(10)
+        logits(11)
+        logits(12)
+        blank(11)
+        presum("V", 7, 1)
+        evacuate(10)
         op_e1("G", 0)
         op_bq("G", 0)
-        presum("V", 6, 2)
+        presum("V", 7, 2)
+        blank(12)
         op_ln(0)
-        quantize_h(6)
-        presum("V", 6, 3)
         quantize_h(7)
-        logits(12)
+        evacuate(11)
         op_ng("G", 0)
+        presum("V", 7, 3)
+        finish("V", 8)
+        store(8)
         logits(13)
-        finish("V", 1)
-        store(1)
         evacuate(12)
         finish("G", 0)
         store(0)
-        exps(11)
-        blank(12)
         logits(14)
+        exps(10)
+        blank(13)
+        finish("G", 1)
+        store(1)
+        evacuate(13)
+        exps(11)
         finish("G", 2)
         store(2)
-        evacuate(13)
-        blank(13)
+        evacuate(14)
         exps(12)
+        finish("G", 3)
+        store(3)
         logits(15)
+        exps(13)
+        blank(14)
+        finish("G", 4)
+        store(4)
+        blank(15)
+        exps(14)
+        evacuate(15)
         finish("G", 5)
         store(5)
-        evacuate(14)
         op_az(1)
-        exps(13)
-        finish("G", 10)
-        store(10)
-        evacuate(15)
-        exps(14)
-        finish("V", 3)
-        store(3)
-        exps(15)
-        finish("V", 4)
-        store(4)
-        finish("V", 6)
+        finish("G", 6)
         store(6)
-        finish("V", 7)
+        exps(15)
+        op_mr(1)
+        finish("G", 7)
         store(7)
         op_ez(1)
-        finish("V", 8)
-        store(8)
-        finish("V", 9)
+        op_bq("V", 1)
+        finish("G", 9)
         store(9)
-        op_mr(1)
-        op_e1("G", 1)
-        op_bq("G", 1)
         op_ln(1)
-        op_ng("G", 1)
-        finish("V", 13)
-        store(13)
-        finish("V", 15)
-        store(15)
-        finish("G", 11)
+        op_ng("V", 1)
+        finish("V", 11)
         store(11)
+        finish("V", 14)
+        store(14)
+        finish("G", 10)
+        store(10)
         finish("G", 12)
         store(12)
-        finish("G", 14)
-        store(14)
+        finish("G", 13)
+        store(13)
+        finish("G", 15)
+        store(15)

@@ -222,6 +222,22 @@ def tile_hybridautoregressivetransducerjoiner_kernel(
             )
 
         hgs = {}
+        hps = {}
+
+        def scale_slot(k, t):
+            if k not in hps:
+                hp = keep.tile([P, 4, 256], BF16, tag="hp%d" % k, align_bytes=64)
+                hps[k] = hp
+            nc.scalar.activation(out=hps[k][:, t, :], in_=tts[k][:, t, :], func=ACT.Copy, scale=gain[:, t : t + 1])
+
+        def group_slots(k):
+            hg = keep.tile([P, 256, 4], BF16, tag="hg", bufs=PAIRS, align_bytes=64)
+            nc.vector.tensor_copy(
+                out=hg[:].rearrange("p (c i) t -> p c t i", i=4),
+                in_=hps[k][:].rearrange("p t (c i) -> p c t i", i=4),
+            )
+            hgs[k] = hg
+
         hqs = {}
 
         def apply_gain(eng, k):
@@ -246,7 +262,7 @@ def tile_hybridautoregressivetransducerjoiner_kernel(
         batch_of = [0,0,0,0,0,0,0,0,0,0,1,1,1,1,1,1]
         zbs = {}
 
-        zmode = "PVSSPPPS"
+        zmode = "SSPVPPSS"
         zsum = {}
 
         def presum(eng, k, step):
@@ -385,7 +401,7 @@ def tile_hybridautoregressivetransducerjoiner_kernel(
             else:
                 nc.gpsimd.tensor_tensor(out=small[("ng", i)][:, c], in0=small[("ln", i)][:, c], in1=small[("mr", i)][:, c], op=ALU.add)
 
-        beng = "GVVVVG"
+        beng = "VVVGVG"
 
         def finish(eng, b):
             o = ots[b // 2][:, b % 2, :]
@@ -415,82 +431,92 @@ def tile_hybridautoregressivetransducerjoiner_kernel(
             else:
                 copy(eng, half_grouped(wp_g, h), half_raw(wp_w, h))
 
-        widen("V", 0)
-        widen("S", 1)
+        widen("S", 0)
+        widen("V", 1)
         transpose_pred()
-        widen("V", 2)
         widen("V", 3)
+        widen("S", 2)
         transpose_enc()
-        copy_pred("V")
-        il_w("S", "wp", 0)
-        copy_enc("V")
+        copy_pred("S")
+        il_w("V", "wp", 1)
+        il_w("V", "we", 1)
+        copy_enc("S")
         il_w("S", "we", 0)
         nc.vector.quantize_mx(out=pred_c[:].bitcast(FP8X4), scales=pred_s[:], in_=pred_g[:])
         nc.vector.quantize_mx(out=enc_c[:].bitcast(FP8X4), scales=enc_s[:], in_=enc_g[:])
-        quantize_half(wp_g, wp_c, wp_s, 0)
-        il_w("S", "wp", 1)
-        il_w("V", "we", 1)
+        quantize_half(wp_g, wp_c, wp_s, 1)
+        quantize_half(we_g, we_c, we_s, 1)
+        il_w("S", "wp", 0)
+        replicate(2, 2)
         quantize_half(we_g, we_c, we_s, 0)
         replicate(0, 2)
-        il_w("S", "wo", 0)
-        quantize_half(we_g, we_c, we_s, 1)
-        quantize_half(wp_g, wp_c, wp_s, 1)
-        first_stage(0, 0)
-        replicate(2, 4)
-        il_w("S", "wo", 1)
-        quantize_half(wo_g, wo_c, wo_s, 0)
-        first_stage(0, 1)
-        replicate(6, 10)
-        first_stage(1, 0)
-        tanh(0, 0)
         first_stage(1, 1)
-        tanh(0, 1)
-        first_stage(2, 0)
-        tanh(1, 0)
-        quantize_half(wo_g, wo_c, wo_s, 1)
-        first_stage(2, 1)
-        apply_gain("V", 0)
+        il_w("S", "wo", 0)
+        replicate(4, 4)
+        first_stage(0, 1)
+        quantize_half(wp_g, wp_c, wp_s, 0)
         tanh(1, 1)
-        first_stage(3, 0)
-        tanh(2, 0)
+        il_w("V", "wo", 1)
+        first_stage(0, 0)
+        tanh(0, 1)
+        replicate(8, 8)
+        first_stage(1, 0)
+        scale_slot(1, 2)
+        tanh(0, 0)
+        first_stage(2, 1)
+        tanh(1, 0)
         first_stage(3, 1)
+        quantize_half(wo_g, wo_c, wo_s, 0)
+        apply_gain("V", 0)
+        presum("S", 0, 0)
+        first_stage(2, 0)
         tanh(2, 1)
-        presum("V", 1, 0)
-        apply_gain("V", 1)
-        blank(0)
-        tanh(3, 0)
-        tanh(3, 1)
-        first_stage(4, 0)
-        quantize_h(0)
-        presum("S", 2, 0)
-        presum("V", 1, 1)
-        presum("S", 3, 0)
+        first_stage(3, 0)
+        presum("S", 1, 0)
+        tanh(2, 0)
         first_stage(4, 1)
-        quantize_h(1)
-        tanh(4, 0)
-        apply_gain("V", 2)
+        presum("V", 0, 1)
+        quantize_half(wo_g, wo_c, wo_s, 1)
+        tanh(3, 0)
+        quantize_h(0)
+        first_stage(4, 0)
+        presum("V", 0, 2)
+        tanh(3, 1)
+        presum("V", 1, 1)
         logits(0)
+        apply_gain("V", 2)
+        scale_slot(1, 3)
         logits(1)
-        tanh(4, 1)
-        logits(2)
+        scale_slot(1, 0)
         first_stage(5, 0)
-        presum("V", 1, 2)
+        scale_slot(1, 1)
+        tanh(4, 0)
         first_stage(5, 1)
-        presum("V", 2, 1)
+        presum("V", 0, 3)
+        tanh(4, 1)
+        blank(4)
+        presum("V", 1, 2)
+        group_slots(1)
         tanh(5, 0)
+        tanh(5, 1)
+        presum("V", 1, 3)
+        blank(0)
         quantize_h(2)
         first_stage(6, 0)
-        presum("V", 1, 3)
-        tanh(5, 1)
-        presum("V", 2, 2)
-        first_stage(6, 1)
-        presum("V", 3, 1)
-        tanh(6, 0)
+        scale_slot(4, 0)
+        quantize_h(1)
+        scale_slot(4, 1)
+        presum("V", 3, 0)
         blank(1)
+        scale_slot(4, 2)
         apply_gain("G", 3)
         evacuate(0)
-        tanh(6, 1)
+        first_stage(6, 1)
+        tanh(6, 0)
         evacuate(1)
+        logits(2)
+        scale_slot(4, 3)
+        blank(2)
         exps(0)
         logits(3)
         evacuate(2)
@@ -498,118 +524,124 @@ def tile_hybridautoregressivetransducerjoiner_kernel(
         exps(1)
         evacuate(3)
         logits(4)
-        apply_gain("G", 4)
-        exps(2)
+        apply_gain("G", 5)
+        tanh(6, 1)
         logits(5)
-        first_stage(7, 1)
+        blank(3)
         evacuate(4)
-        tanh(7, 0)
-        blank(2)
+        exps(2)
+        first_stage(7, 1)
         evacuate(5)
         exps(3)
-        blank(3)
-        blank(8)
-        tanh(7, 1)
-        presum("V", 2, 3)
+        blank(5)
         exps(4)
-        presum("V", 3, 2)
-        blank(9)
+        presum("V", 3, 1)
+        tanh(7, 0)
+        blank(8)
         quantize_h(3)
+        group_slots(4)
         exps(5)
+        presum("V", 3, 2)
+        tanh(7, 1)
+        logits(6)
+        quantize_h(5)
         quantize_h(4)
+        presum("S", 6, 0)
+        logits(7)
         presum("V", 3, 3)
         presum("S", 7, 0)
-        apply_gain("V", 5)
-        logits(6)
-        logits(7)
-        logits(8)
+        scale_slot(7, 0)
         apply_gain("G", 6)
         evacuate(6)
-        blank(4)
-        blank(5)
-        evacuate(7)
+        logits(8)
+        scale_slot(7, 1)
         blank(6)
-        exps(6)
-        logits(9)
-        evacuate(8)
+        scale_slot(7, 2)
+        evacuate(7)
         blank(7)
+        scale_slot(7, 3)
+        logits(9)
+        exps(6)
+        evacuate(8)
+        blank(9)
         exps(7)
-        blank(10)
         evacuate(9)
-        op_az(0)
         exps(8)
-        quantize_h(5)
-        quantize_h(6)
-        op_ez(0)
-        exps(9)
-        op_mr(0)
-        apply_gain("V", 7)
+        presum("V", 6, 1)
         logits(10)
+        quantize_h(6)
+        op_az(0)
+        exps(9)
         logits(11)
-        logits(12)
-        blank(11)
+        op_mr(0)
+        presum("V", 6, 2)
+        blank(10)
         presum("V", 7, 1)
-        evacuate(10)
-        op_e1("G", 0)
-        op_bq("G", 0)
+        op_ez(0)
+        group_slots(7)
+        presum("V", 6, 3)
+        op_bq("V", 0)
+        logits(12)
         presum("V", 7, 2)
-        blank(12)
-        op_ln(0)
+        blank(11)
         quantize_h(7)
-        evacuate(11)
-        op_ng("G", 0)
+        op_ln(0)
+        evacuate(10)
+        op_ng("V", 0)
         presum("V", 7, 3)
-        finish("V", 8)
-        store(8)
+        evacuate(11)
         logits(13)
-        evacuate(12)
         finish("G", 0)
         store(0)
-        logits(14)
+        blank(12)
         exps(10)
         blank(13)
+        evacuate(12)
         finish("G", 1)
         store(1)
-        evacuate(13)
-        exps(11)
-        finish("G", 2)
-        store(2)
-        evacuate(14)
-        exps(12)
-        finish("G", 3)
-        store(3)
-        logits(15)
-        exps(13)
         blank(14)
+        exps(11)
         finish("G", 4)
         store(4)
+        logits(14)
+        evacuate(13)
         blank(15)
-        exps(14)
-        evacuate(15)
+        exps(12)
         finish("G", 5)
         store(5)
+        logits(15)
+        evacuate(14)
         op_az(1)
+        exps(13)
         finish("G", 6)
         store(6)
-        exps(15)
-        op_mr(1)
-        finish("G", 7)
-        store(7)
+        evacuate(15)
         op_ez(1)
-        op_bq("V", 1)
-        finish("G", 9)
+        exps(14)
+        finish("V", 2)
+        store(2)
+        finish("V", 3)
+        store(3)
+        exps(15)
+        finish("V", 7)
+        store(7)
+        finish("V", 8)
+        store(8)
+        finish("V", 9)
         store(9)
+        op_mr(1)
+        op_bq("V", 1)
         op_ln(1)
         op_ng("V", 1)
         finish("V", 11)
         store(11)
+        finish("S", 12)
+        store(12)
         finish("V", 14)
         store(14)
+        finish("S", 13)
+        store(13)
         finish("G", 10)
         store(10)
-        finish("G", 12)
-        store(12)
-        finish("G", 13)
-        store(13)
-        finish("G", 15)
+        finish("S", 15)
         store(15)

from contextlib import ExitStack

import concourse.mybir as mybir
from concourse.masks import make_identity

F32 = mybir.dt.float32
BF16 = mybir.dt.bfloat16
I32 = mybir.dt.int32
U8 = mybir.dt.uint8
FP8 = mybir.dt.float8_e4m3fn
FP8X4 = mybir.dt.float8_e4m3fn_x4
ALU = mybir.AluOpType
ACT = mybir.ActivationFunctionType

P = 128
ZN = 32
ZNB = 10
B, T, U, K, J, V = 16, 16, 8, 512, 512, 512
ROWS = B * T * U
PAIRS = B // 2

FLOPS = 2 * K * J * (B * T + B * U) + 2 * ROWS * J * V + 2 * ROWS * J


def tile_hybridautoregressivetransducerjoiner_kernel(
    tc, enc, pred, we, wp_bytes, wp_scale, gj, wo, wb, out
):
    nc = tc.nc

    with ExitStack() as ctx:
        keep = ctx.enter_context(tc.tile_pool(name="keep", bufs=1))
        work = ctx.enter_context(tc.tile_pool(name="work", bufs=3))
        psum = ctx.enter_context(tc.psum_pool(name="psum", bufs=1))
        ctx.enter_context(tc.manual_schedule())

        wp_raw = keep.tile([P, 4, J], U8, align_bytes=64)
        nc.sync.dma_start(out=wp_raw[:], in_=wp_bytes.rearrange("(p j) n -> p j n", j=4))
        pred_raw = keep.tile([P, K], BF16, align_bytes=64)
        nc.sync.dma_start(out=pred_raw[:], in_=pred.rearrange("b u k -> (b u) k"))
        enc_raw = keep.tile([P, 2, K], BF16, align_bytes=64)
        nc.sync.dma_start(out=enc_raw[:], in_=enc.rearrange("b i k -> (b i) k").rearrange("(p e) k -> p e k", e=2))
        we_raw = keep.tile([P, 4, J], BF16, align_bytes=64)
        nc.sync.dma_start(out=we_raw[:], in_=we.rearrange("(p j) n -> p j n", j=4))
        wo_raw = keep.tile([P, 4, V], BF16, align_bytes=64)
        nc.sync.dma_start(out=wo_raw[:], in_=wo.rearrange("(p j) n -> p j n", j=4))
        wps = keep.tile([P, 4], F32)
        nc.scalar.dma_start(out=wps[:], in_=wp_scale.rearrange("(p j) o -> p (j o)", j=4))
        gj_raw = keep.tile([P, 4], BF16)
        nc.scalar.dma_start(out=gj_raw[:], in_=gj.rearrange("(p t) -> p t", t=4))
        wb_raw = keep.tile([P, 4], BF16)
        nc.scalar.dma_start(out=wb_raw[:], in_=wb.rearrange("(p t) -> p t", t=4))

        warm = keep.tile([P, 1], F32)
        nc.vector.memset(warm[:], 0.0)
        warm_out = keep.tile([P, 1], F32)
        nc.scalar.activation(out=warm_out[:], in_=warm[:], func=ACT.Exp)
        ones = keep.tile([P, 1], F32)
        nc.gpsimd.memset(ones[:], 1.0)
        ident = keep.tile([P, P], F32)
        make_identity(nc, ident[:])
        enc_s = keep.tile([P, B * T], U8, align_bytes=64)
        nc.gpsimd.memset(enc_s[:].bitcast(I32), 0)
        pred_s = keep.tile([P, B * U * 4], U8, align_bytes=64)
        nc.gpsimd.memset(pred_s[:].bitcast(I32), 0)
        gain = keep.tile([P, 4], F32)
        nc.gpsimd.tensor_copy(out=gain[:], in_=gj_raw[:])
        wbf = keep.tile([P, 4], F32)
        nc.gpsimd.tensor_copy(out=wbf[:], in_=wb_raw[:])
        wbr = keep.tile([P, 4, ZN], F32)
        nc.gpsimd.tensor_copy(out=wbr[:], in_=wbf[:].unsqueeze(2).to_broadcast([P, 4, ZN]))

        enc_g = keep.tile([P, B * T * 4], BF16, align_bytes=64)
        pred_g = keep.tile([P, B * U * 16], BF16, align_bytes=64)
        enc_c = keep.tile([P, B * T], I32, align_bytes=64)
        pred_c = keep.tile([P, B * U * 4], I32, align_bytes=64)
        wp_w = keep.tile([P, 4, J], BF16, align_bytes=64)
        xs = {}

        def copy(eng, out, in_):
            if eng == "V":
                nc.vector.tensor_copy(out=out, in_=in_)
            else:
                nc.scalar.copy(out=out, in_=in_)

        def transpose_enc():
            xe = psum.tile([P, 2, 2, P], F32, tag="s1", bufs=4)
            for e in range(2):
                words = enc_raw[:, e, :].bitcast(F32)
                for u in range(2):
                    nc.tensor.transpose(xe[:, e, u, :], words[:, u : K // 2 : 2], ident[:])
            xs["e"] = xe

        def transpose_pred():
            xp = psum.tile([P, 2, P], F32, tag="lg", bufs=3)
            pwords = pred_raw[:].bitcast(F32)
            for u in range(2):
                nc.tensor.transpose(xp[:, u, :], pwords[:, u : K // 2 : 2], ident[:])
            xs["p"] = xp

        def copy_enc(eng):
            copy(
                eng,
                enc_g[:].bitcast(F32).rearrange("q (r e u) -> q r e u", e=2, u=2),
                xs["e"][:].rearrange("q e u r -> q r e u"),
            )

        def copy_pred(eng):
            copy(
                eng,
                pred_g[:].bitcast(F32).rearrange("q (r l u) -> q r l u", l=4, u=2),
                xs["p"][:].rearrange("q u r -> q r u").unsqueeze(2).to_broadcast([P, P, 4, 2]),
            )

        def widen(eng, j):
            if eng == "V":
                nc.vector.tensor_scalar(
                    out=wp_w[:, j, :],
                    in0=wp_raw[:, j, :].bitcast(FP8),
                    scalar1=wps[:, j : j + 1],
                    scalar2=None,
                    op0=ALU.mult,
                )
            else:
                nc.scalar.activation(
                    out=wp_w[:, j, :], in_=wp_raw[:, j, :].bitcast(FP8), func=ACT.Copy, scale=wps[:, j : j + 1]
                )

        enc_rc = keep.tile([P, ROWS], I32, align_bytes=64)
        enc_rs = keep.tile([P, ROWS], U8, align_bytes=64)
        pred_rc = keep.tile([P, ROWS], I32, align_bytes=64)
        pred_rs = keep.tile([P, ROWS], U8, align_bytes=64)

        def replicate(b0, nb):
            nc.vector.tensor_copy(
                out=enc_rc[:, b0 * 128 : (b0 + nb) * 128].rearrange("p (a u l) -> p a u l", u=8, l=4),
                in_=enc_c[:, b0 * 16 : (b0 + nb) * 16]
                .rearrange("p (a l) -> p a l", l=4)
                .unsqueeze(2)
                .to_broadcast([P, nb * 4, 8, 4]),
            )
            nc.vector.tensor_copy(
                out=enc_rs[:].bitcast(I32)[:, b0 * 32 : (b0 + nb) * 32].rearrange("p (a u) -> p a u", u=8),
                in_=enc_s[:].bitcast(I32)[:, b0 * 4 : (b0 + nb) * 4].unsqueeze(2).to_broadcast([P, nb * 4, 8]),
            )
            nc.vector.tensor_copy(
                out=pred_rc[:, b0 * 128 : (b0 + nb) * 128].rearrange("p (b i w) -> p b i w", i=4, w=32),
                in_=pred_c[:, b0 * 32 : (b0 + nb) * 32]
                .rearrange("p (b w) -> p b w", w=32)
                .unsqueeze(2)
                .to_broadcast([P, nb, 4, 32]),
            )
            nc.vector.tensor_copy(
                out=pred_rs[:].bitcast(I32)[:, b0 * 32 : (b0 + nb) * 32].rearrange("p (b i u) -> p b i u", i=4, u=8),
                in_=pred_s[:]
                .bitcast(I32)[:, b0 * 8 : (b0 + nb) * 8]
                .rearrange("p (b u) -> p b u", u=8)
                .unsqueeze(2)
                .to_broadcast([P, nb, 4, 8]),
            )

        we_g = keep.tile([P, 4 * J], BF16, align_bytes=64)
        wp_g = keep.tile([P, 4 * J], BF16, align_bytes=64)
        we_c = keep.tile([P, J], I32, align_bytes=64)
        we_s = keep.tile([P, J], U8, align_bytes=64)
        wp_c = keep.tile([P, J], I32, align_bytes=64)
        wp_s = keep.tile([P, J], U8, align_bytes=64)
        wo_g = keep.tile([P, 4 * V], BF16, align_bytes=64)
        wo_c = keep.tile([P, V], I32, align_bytes=64)
        wo_s = keep.tile([P, V], U8, align_bytes=64)

        def half_grouped(grouped, h):
            return grouped[:, h * 1024 : (h + 1) * 1024].rearrange("p (t m j) -> p t m j", t=2, j=4)

        def half_raw(raw, h):
            return raw[:].rearrange("p j (m t) -> p t m j", t=4)[:, 2 * h : 2 * h + 2]

        def quantize_half(grouped, codes, scales, h):
            nc.vector.quantize_mx(
                out=codes[:, h * 256 : (h + 1) * 256].bitcast(FP8X4),
                scales=scales[:, h * 256 : (h + 1) * 256],
                in_=grouped[:, h * 1024 : (h + 1) * 1024],
            )

        tts = []
        for k in range(PAIRS):
            tt = keep.tile([P, 4, 256], F32, tag="tt", bufs=PAIRS, align_bytes=64)
            tts.append(tt)

        s1s = {}

        def first_stage(k, h):
            s1 = psum.tile([P, 2, 256], F32, tag="s1", bufs=4)
            s1s[(k, h)] = s1
            cols = slice(k * 256, (k + 1) * 256)
            for i in range(2):
                t = 2 * h + i
                ch = slice(t * 128, (t + 1) * 128)
                nc.tensor.matmul_mx(
                    out=s1[:, i, :],
                    lhsT=we_c[:, ch].bitcast(FP8X4),
                    lhsT_scale=we_s[:, ch],
                    rhs=enc_rc[:, cols].bitcast(FP8X4),
                    rhs_scale=enc_rs[:, cols],
                    start=True,
                    stop=False,
                )
                nc.tensor.matmul_mx(
                    out=s1[:, i, :],
                    lhsT=wp_c[:, ch].bitcast(FP8X4),
                    lhsT_scale=wp_s[:, ch],
                    rhs=pred_rc[:, cols].bitcast(FP8X4),
                    rhs_scale=pred_rs[:, cols],
                    start=False,
                    stop=True,
                )

        def tanh(k, h):
            nc.scalar.activation(
                out=tts[k][:, 2 * h : 2 * h + 2, :].rearrange("p t (a l u) -> p (t a) l u", l=4, u=8),
                in_=s1s[(k, h)][:].rearrange("p t (a u l) -> p (t a) l u", l=4, u=8),
                func=ACT.Tanh,
            )

        hgs = {}
        hps = {}

        def scale_slot(k, t):
            if k not in hps:
                hp = keep.tile([P, 4, 256], BF16, tag="hp%d" % k, align_bytes=64)
                hps[k] = hp
            nc.scalar.activation(out=hps[k][:, t, :], in_=tts[k][:, t, :], func=ACT.Copy, scale=gain[:, t : t + 1])

        def group_slots(k):
            hg = keep.tile([P, 256, 4], BF16, tag="hg", bufs=PAIRS, align_bytes=64)
            nc.vector.tensor_copy(
                out=hg[:].rearrange("p (c i) t -> p c t i", i=4),
                in_=hps[k][:].rearrange("p t (c i) -> p c t i", i=4),
            )
            hgs[k] = hg

        hqs = {}

        def apply_gain(eng, k):
            hg = keep.tile([P, 256, 4], BF16, tag="hg", bufs=PAIRS, align_bytes=64)
            (nc.vector if eng == "V" else nc.gpsimd).tensor_tensor(
                out=hg[:].rearrange("p (c i) t -> p c t i", i=4),
                in0=tts[k][:].rearrange("p t (c i) -> p c t i", i=4),
                in1=gain[:].unsqueeze(1).unsqueeze(3).to_broadcast([P, 64, 4, 4]),
                op=ALU.mult,
            )
            hgs[k] = hg

        def quantize_h(k):
            hc = keep.tile([P, 256], I32, tag="hc", bufs=PAIRS, align_bytes=64)
            hs = keep.tile([P, 256], U8, tag="hs", bufs=PAIRS, align_bytes=64)
            nc.vector.quantize_mx(
                out=hc[:].bitcast(FP8X4), scales=hs[:], in_=hgs[k][:].rearrange("p n t -> p (n t)")
            )
            hqs[k] = (hc, hs)

        batches = [[0,10],[10,16]]
        batch_of = [0,0,0,0,0,0,0,0,0,0,1,1,1,1,1,1]
        zbs = {}

        zmode = "SSPVPPSS"
        zsum = {}

        def presum(eng, k, step):
            if step == 0:
                zr = keep.tile([P, 256], F32, tag="zr%d" % k, align_bytes=64)
                zsum[k] = zr
            z = zsum[k][:]
            x = tts[k][:, step, :]
            w = wbf[:, step : step + 1]
            if step == 0:
                if eng == "S":
                    nc.scalar.activation(out=z, in_=x, func=ACT.Copy, scale=w)
                else:
                    nc.vector.tensor_scalar(out=z, in0=x, scalar1=w, scalar2=None, op0=ALU.mult)
            else:
                nc.vector.scalar_tensor_tensor(out=z, in0=x, scalar=w, in1=z, op0=ALU.mult, op1=ALU.add)

        def blank(b):
            i = batch_of[b]
            if i not in zbs:
                zb = psum.tile([P, batches[i][1] - batches[i][0], ZN], F32, tag="zb" if i == 0 else "s1", bufs=1 if i == 0 else 4)
                zbs[i] = zb
            k, c = b // 2, b % 2
            col = b - batches[i][0]
            cols = slice(c * 128, (c + 1) * 128)
            n = ZN if b >= ZNB else 1
            if zmode[k] == "P":
                for t in range(4):
                    nc.tensor.matmul(
                        out=zbs[i][:, col, 0:n],
                        lhsT=tts[k][:, t, cols],
                        rhs=wbr[:, t, 0:n],
                        start=(t == 0),
                        stop=(t == 3),
                    )
            else:
                nc.tensor.matmul(
                    out=zbs[i][:, col, 0:1], lhsT=zsum[k][:, cols], rhs=ones[:], start=True, stop=True
                )

        nm = keep.tile([P, B], F32)
        ssum = keep.tile([P, B], F32)
        lgs = {}
        ots = {}

        def logits(b):
            hc, hs = hqs[b // 2]
            c = b % 2
            cols = slice(c * 128, (c + 1) * 128)
            lg = psum.tile([P, V], F32, tag="lg", bufs=3)
            nc.tensor.matmul_mx(
                out=lg[:],
                lhsT=hc[:, cols].bitcast(FP8X4),
                lhsT_scale=hs[:, cols],
                rhs=wo_c[:].bitcast(FP8X4),
                rhs_scale=wo_s[:],
                start=True,
                stop=True,
            )
            lgs[b] = lg
            if c == 0:
                ot = keep.tile([P, 2, V], F32, tag="ot", bufs=PAIRS, align_bytes=64)
                ots[b // 2] = ot

        def evacuate(b):
            nc.vector.tensor_scalar(
                out=ots[b // 2][:, b % 2, :],
                in0=lgs[b][:],
                scalar1=-1.0,
                scalar2=None,
                op0=ALU.mult,
                op1=ALU.min,
                accum_out=nm[:, b : b + 1],
            )

        def exps(b):
            junk = work.tile([P, V], F32)
            nc.scalar.activation(
                out=junk[:],
                in_=ots[b // 2][:, b % 2, :],
                func=ACT.Exp,
                bias=nm[:, b : b + 1],
                scale=-1.0,
                accum_out=ssum[:, b : b + 1],
            )

        small = {}
        for i in range(len(batches)):
            for what in ("az", "ez", "e1", "mr", "qq", "ln", "ng"):
                piece = keep.tile([P, B], F32, tag="%s%d" % (what, i), align_bytes=64)
                small[(what, i)] = piece

        engines = {"V": nc.vector, "G": nc.gpsimd}

        def cols_of(i):
            return slice(batches[i][0], batches[i][1])

        def op_az(i):
            nc.scalar.activation(out=small[("az", i)][:, cols_of(i)], in_=zbs[i][:, :, 0], func=ACT.Abs)

        def op_ez(i):
            nc.scalar.activation(out=small[("ez", i)][:, cols_of(i)], in_=small[("az", i)][:, cols_of(i)], func=ACT.Exp, scale=-1.0)

        def op_mr(i):
            nc.vector.scalar_tensor_tensor(
                out=small[("mr", i)][:, cols_of(i)], in0=zbs[i][:, :, 0], scalar=0.0, in1=nm[:, cols_of(i)], op0=ALU.max, op1=ALU.subtract
            )

        def op_e1(eng, i):
            engines[eng].tensor_scalar(
                out=small[("e1", i)][:, cols_of(i)], in0=small[("ez", i)][:, cols_of(i)], scalar1=1.0, scalar2=1.0, op0=ALU.mult, op1=ALU.add
            )

        def op_bq(eng, i):
            c = cols_of(i)
            if eng == "V":
                nc.vector.scalar_tensor_tensor(
                    out=small[("qq", i)][:, c], in0=small[("ez", i)][:, c], scalar=1.0, in1=ssum[:, c], op0=ALU.add, op1=ALU.mult
                )
            else:
                nc.gpsimd.tensor_tensor(out=small[("qq", i)][:, c], in0=small[("e1", i)][:, c], in1=ssum[:, c], op=ALU.mult)

        def op_ln(i):
            c = cols_of(i)
            if batches[i][1] - batches[i][0] == 1:
                nc.scalar.activation(out=small[("ln", i)][:, c], in_=ssum[:, c], func=ACT.Ln, scale=small[("e1", i)][:, c])
            else:
                nc.scalar.activation(out=small[("ln", i)][:, c], in_=small[("qq", i)][:, c], func=ACT.Ln)

        def op_ng(eng, i):
            c = cols_of(i)
            if eng == "V":
                nc.vector.scalar_tensor_tensor(
                    out=small[("ng", i)][:, c], in0=small[("ln", i)][:, c], scalar=-1.0, in1=small[("mr", i)][:, c], op0=ALU.mult, op1=ALU.subtract
                )
            else:
                nc.gpsimd.tensor_tensor(out=small[("ng", i)][:, c], in0=small[("ln", i)][:, c], in1=small[("mr", i)][:, c], op=ALU.add)

        beng = "VVVGVG"

        def finish(eng, b):
            o = ots[b // 2][:, b % 2, :]
            n = small[("ng", batch_of[b])][:, b : b + 1]
            negated = beng[batch_of[b]] == "V"
            if eng == "S":
                nc.scalar.activation(out=o, in_=o, func=ACT.Identity, bias=n, scale=-1.0)
            elif negated:
                engines[eng].tensor_scalar(out=o, in0=o, scalar1=-1.0, scalar2=n, op0=ALU.mult, op1=ALU.add)
            else:
                engines[eng].tensor_scalar(out=o, in0=o, scalar1=n, scalar2=-1.0, op0=ALU.add, op1=ALU.mult)

        rows = out.rearrange("b i u v -> (b i u) v").rearrange("(k c p) v -> k p c v", c=2, p=P)

        def store(b):
            nc.sync.dma_start(out=rows[b // 2][:, b % 2, :], in_=ots[b // 2][:, b % 2, :])

        def il_w(eng, which, h):
            if which == "wo":
                copy(
                    eng,
                    wo_g[:, h * 1024 : (h + 1) * 1024].rearrange("p (c i j) -> p c j i", i=4, j=4),
                    wo_raw[:, :, h * 256 : (h + 1) * 256].rearrange("p j (c i) -> p c j i", i=4),
                )
            elif which == "we":
                copy(eng, half_grouped(we_g, h), half_raw(we_raw, h))
            else:
                copy(eng, half_grouped(wp_g, h), half_raw(wp_w, h))

        widen("S", 0)
        widen("V", 1)
        transpose_pred()
        widen("V", 3)
        widen("S", 2)
        transpose_enc()
        copy_pred("S")
        il_w("V", "wp", 1)
        il_w("V", "we", 1)
        copy_enc("S")
        il_w("S", "we", 0)
        nc.vector.quantize_mx(out=pred_c[:].bitcast(FP8X4), scales=pred_s[:], in_=pred_g[:])
        nc.vector.quantize_mx(out=enc_c[:].bitcast(FP8X4), scales=enc_s[:], in_=enc_g[:])
        quantize_half(wp_g, wp_c, wp_s, 1)
        quantize_half(we_g, we_c, we_s, 1)
        il_w("S", "wp", 0)
        replicate(2, 2)
        quantize_half(we_g, we_c, we_s, 0)
        replicate(0, 2)
        first_stage(1, 1)
        il_w("S", "wo", 0)
        replicate(4, 4)
        first_stage(0, 1)
        quantize_half(wp_g, wp_c, wp_s, 0)
        tanh(1, 1)
        il_w("V", "wo", 1)
        first_stage(0, 0)
        tanh(0, 1)
        replicate(8, 8)
        first_stage(1, 0)
        scale_slot(1, 2)
        tanh(0, 0)
        first_stage(2, 1)
        tanh(1, 0)
        first_stage(3, 1)
        quantize_half(wo_g, wo_c, wo_s, 0)
        apply_gain("V", 0)
        presum("S", 0, 0)
        first_stage(2, 0)
        tanh(2, 1)
        first_stage(3, 0)
        presum("S", 1, 0)
        tanh(2, 0)
        first_stage(4, 1)
        presum("V", 0, 1)
        quantize_half(wo_g, wo_c, wo_s, 1)
        tanh(3, 0)
        quantize_h(0)
        first_stage(4, 0)
        presum("V", 0, 2)
        tanh(3, 1)
        presum("V", 1, 1)
        logits(0)
        apply_gain("V", 2)
        scale_slot(1, 3)
        logits(1)
        scale_slot(1, 0)
        first_stage(5, 0)
        scale_slot(1, 1)
        tanh(4, 0)
        first_stage(5, 1)
        presum("V", 0, 3)
        tanh(4, 1)
        blank(4)
        presum("V", 1, 2)
        group_slots(1)
        tanh(5, 0)
        tanh(5, 1)
        presum("V", 1, 3)
        blank(0)
        quantize_h(2)
        first_stage(6, 0)
        scale_slot(4, 0)
        quantize_h(1)
        scale_slot(4, 1)
        presum("V", 3, 0)
        blank(1)
        scale_slot(4, 2)
        apply_gain("G", 3)
        evacuate(0)
        first_stage(6, 1)
        tanh(6, 0)
        evacuate(1)
        logits(2)
        scale_slot(4, 3)
        blank(2)
        exps(0)
        logits(3)
        evacuate(2)
        first_stage(7, 0)
        exps(1)
        evacuate(3)
        logits(4)
        apply_gain("G", 5)
        tanh(6, 1)
        logits(5)
        blank(3)
        evacuate(4)
        exps(2)
        first_stage(7, 1)
        evacuate(5)
        exps(3)
        blank(5)
        exps(4)
        presum("V", 3, 1)
        tanh(7, 0)
        blank(8)
        quantize_h(3)
        group_slots(4)
        exps(5)
        presum("V", 3, 2)
        tanh(7, 1)
        logits(6)
        quantize_h(5)
        quantize_h(4)
        presum("S", 6, 0)
        logits(7)
        presum("V", 3, 3)
        presum("S", 7, 0)
        scale_slot(7, 0)
        apply_gain("G", 6)
        evacuate(6)
        logits(8)
        scale_slot(7, 1)
        blank(6)
        scale_slot(7, 2)
        evacuate(7)
        blank(7)
        scale_slot(7, 3)
        logits(9)
        exps(6)
        evacuate(8)
        blank(9)
        exps(7)
        evacuate(9)
        exps(8)
        presum("V", 6, 1)
        logits(10)
        quantize_h(6)
        op_az(0)
        exps(9)
        logits(11)
        op_mr(0)
        presum("V", 6, 2)
        blank(10)
        presum("V", 7, 1)
        op_ez(0)
        group_slots(7)
        presum("V", 6, 3)
        op_bq("V", 0)
        logits(12)
        presum("V", 7, 2)
        blank(11)
        quantize_h(7)
        op_ln(0)
        evacuate(10)
        op_ng("V", 0)
        presum("V", 7, 3)
        evacuate(11)
        logits(13)
        finish("G", 0)
        store(0)
        blank(12)
        exps(10)
        blank(13)
        evacuate(12)
        finish("G", 1)
        store(1)
        blank(14)
        exps(11)
        finish("G", 4)
        store(4)
        logits(14)
        evacuate(13)
        blank(15)
        exps(12)
        finish("G", 5)
        store(5)
        logits(15)
        evacuate(14)
        op_az(1)
        exps(13)
        finish("G", 6)
        store(6)
        evacuate(15)
        op_ez(1)
        exps(14)
        finish("V", 2)
        store(2)
        finish("V", 3)
        store(3)
        exps(15)
        finish("V", 7)
        store(7)
        finish("V", 8)
        store(8)
        finish("V", 9)
        store(9)
        op_mr(1)
        op_bq("V", 1)
        op_ln(1)
        op_ng("V", 1)
        finish("V", 11)
        store(11)
        finish("S", 12)
        store(12)
        finish("V", 14)
        store(14)
        finish("S", 13)
        store(13)
        finish("G", 10)
        store(10)
        finish("S", 15)
        store(15)
